import numpy as np, ml_dtypes
CORES = [50,52,122,124]
N = 4
import mx_ref
NC, G = 512, 2
C = np.float32(0.047)
BF = ml_dtypes.bfloat16
def cut(t, i, w=512):
    return t[:, w * i:w * i + w]
def tile(rs):
    return np.stack(rs, axis=2).reshape(128, -1).astype(BF)
def fold(P):
    return [f(p, axis=0) * C for p in P for f in (np.max, np.min)]
def setup_inputs(rng):
    def f(*shape):
        return mx_ref.flush((rng.standard_normal(shape, dtype=np.float32) * np.exp2(rng.integers(-2, 3, shape[:-1] + (1,)))).astype(BF))
    return {"x": f(N, 128, 4 * NC), "w1": f(N, 128, G * 512), "w2": f(N, 128, 2 * 512)}
def setup_inputs_blocks(rng):
    d = setup_inputs(rng)
    for k in ("x", "w1", "w2"): d[k] = mx_ref.spread(d[k], rng, 4)
    return d
def setup_inputs_wide(rng):
    d = setup_inputs(rng)
    for k in ("x", "w1", "w2"): d[k] = mx_ref.flush((d[k].astype(np.float32) * np.exp2(rng.integers(-8, 9, (N, 1, 1))).astype(np.float32)).astype(BF))
    return d
def reference(x, w1, w2, own=None):
    X = [mx_ref.quantize(x[j]) for j in range(N)]
    h = np.stack([tile(fold([[mx_ref.matmul(mx_ref.quantize(cut(w1[r], i)), X[j]) for j in range(N)] for i in range(G)])) for r in range(N)])
    use = h if own is None else own["h"]
    H = [mx_ref.quantize(use[j]) for j in range(N)]
    y = np.zeros((N, 128, NC), np.float32)
    for r in range(N):
        y[r] = mx_ref.matmul(mx_ref.quantize(cut(w2[r], 0)), H[r]) + mx_ref.matmul(mx_ref.quantize(cut(w2[r], 1)), H[(r + 1) % N])
    return {"h": h, "y": y}

@@ -1,0 +1,371 @@
+import numpy as np
+from concourse.bass import DstId, RemoteDMATransfer
+from concourse.mybir import dt, AluOpType, ActivationFunctionType
+
+N = 4
+NC = 512
+CH = [256, 256]
+K = len(CH)
+OFF = [sum(CH[:k]) for k in range(K + 1)]
+WHOLE = True
+OWNER_FAR = "fwd"
+OTHER_FAR = "gate"
+NEAR_FEED = "direct"
+FUSE_PASS = True
+H_STORE_LAST = True
+V_SCALES = True
+FAR_ENG = 16
+NEAR_ENG = 16
+NPAIR = (8 - K) // 2
+CONST = float(np.float32(0.047))
+
+SCRATCH = {
+    "xb": ("sbuf", [128, 4 * NC], "bfloat16"),
+    "w1b": ("sbuf", [128, 1024], "bfloat16"),
+    "w2b": ("sbuf", [128, 1024], "bfloat16"),
+    "w1q": ("sbuf", [128, 256], "float8_e4m3fn_x4"),
+    "w1s": ("sbuf", [128, 256], "uint8"),
+    "w2q": ("sbuf", [128, 256], "float8_e4m3fn_x4"),
+    "w2s": ("sbuf", [128, 256], "uint8"),
+    "hb": ("sbuf", [128, 4 * NC], "bfloat16"),
+    "hq": ("sbuf", [128, NC], "float8_e4m3fn_x4"),
+    "hs": ("sbuf", [128, NC], "uint8"),
+    "hqi": ("sbuf", [128, NC], "float8_e4m3fn_x4"),
+    "hsi": ("sbuf", [128, NC], "uint8"),
+    "yb": ("sbuf", [128, NC], "float32"),
+    "ps": ("psum", [128, 8 * 512], "float32"),
+}
+for _j in range(N):
+    SCRATCH["xq%d" % _j] = ("sbuf", [128, NC], "float8_e4m3fn_x4")
+    SCRATCH["xs%d" % _j] = ("sbuf", [128, NC], "uint8")
+for _i in range(2):
+    for _nm in ("acc", "mx", "mn"):
+        SCRATCH["%s%d" % (_nm, _i)] = ("sbuf", [128, NC], "float32")
+
+SEMAPHORES = (["lw1", "lw2", "qw1", "qw2", "ls", "sth", "sty"]
+              + ["%s%d" % (p, k) for p in ("lx", "qx", "b", "hsc", "qh", "hl", "ym", "ye") for k in range(K)]
+              + ["%s%d_%d" % (p, j, k) for p in ("c", "s") for j in range(N) for k in range(K)]
+              + ["%s%d" % (p, b) for p in ("mm", "rel") for b in range(2 * NPAIR)])
+
+
+def _bits(m):
+    return [e for e in range(16) if (m >> e) & 1]
+
+
+def _pow2(v):
+    p = 1
+    while 2 * p <= v:
+        p *= 2
+    return p
+
+
+def _tomask(engines):
+    m = 0
+    for e in engines:
+        m |= 1 << e
+    return m
+
+
+def _split(topo, src, dsts):
+    far = [i for i, d in enumerate(dsts) if topo.chip(d) != topo.chip(src)]
+    near = [i for i, d in enumerate(dsts) if topo.chip(d) == topo.chip(src)]
+    out = [None] * len(dsts)
+    taken = []
+    if far:
+        pool = _bits(topo.mask(src, dsts[far[0]]))
+        c = min(_pow2(len(pool) // len(far)), FAR_ENG)
+        for n, i in enumerate(far):
+            out[i] = pool[c * n:c * n + c]
+        taken = pool
+    if near:
+        pool = [e for e in _bits(topo.mask(src, dsts[near[0]])) if e not in taken]
+        c = min(_pow2(len(pool) // len(near)), NEAR_ENG)
+        sizes = [c] * len(near)
+        for n in range(len(near)):
+            if sum(sizes) + sizes[n] <= len(pool) and 2 * sizes[n] <= NEAR_ENG:
+                sizes[n] *= 2
+        at = 0
+        for i, s in zip(near, sizes):
+            out[i] = pool[at:at + s]
+            at += s
+    return out
+
+
+def _plan(T, topo):
+    cores = list(T.cores)
+    everyone = range(topo.CORES_PER_CHIP * topo.CHIPS)
+    busy = list(cores)
+    tree, due = [], []
+
+    def hurried(d):
+        return topo.chip(cores[(cores.index(d) - 1) % N]) != topo.chip(d)
+
+    def helper(c, d, at_mate):
+        if at_mate:
+            q = [q for q in everyone if q not in busy and topo.mates(topo.chip(q), topo.chip(d))
+                 and topo.same_plane(topo.chip(q), topo.chip(c)) and topo.die(q) == topo.die(c)
+                 and topo.may_write(q, d)][0]
+        else:
+            q = [q for q in everyone if q not in busy and topo.chip(q) == topo.chip(c)
+                 and topo.die(q) == topo.die(c) and topo.may_write(q, d)][0]
+        busy.append(q)
+        return q
+
+    for c in cores:
+        kids = {c: []}
+        near = [d for d in cores if d != c and topo.chip(d) == topo.chip(c)]
+        far = sorted([d for d in cores if topo.chip(d) != topo.chip(c)], key=lambda d: not hurried(d))
+        if all(topo.may_write(c, d) for d in far):
+            kids[c] += near
+            if OWNER_FAR == "fwd":
+                kids[c].append(far[0])
+                kids[far[0]] = far[1:]
+            else:
+                kids[c] += far
+        elif OTHER_FAR == "chain":
+            kids = {c: near, [d for d in near if topo.may_write(d, far[0])][0]: [far[0]], far[0]: [far[1]]}
+        else:
+            h1 = helper(c, far[0], False)
+            kids[c].append(h1)
+            kids[h1] = [far[0]]
+            if OTHER_FAR in ("mate", "same"):
+                h2 = helper(c, far[1], OTHER_FAR == "mate")
+                kids[c].append(h2)
+                kids[h2] = [far[1]]
+            elif OTHER_FAR == "h1dup":
+                kids[h1].append(far[1])
+            elif OTHER_FAR == "gate":
+                kids[[d for d in near if topo.may_write(d, far[1])][0]] = [far[1]]
+            else:
+                kids[far[0]] = [far[1]]
+            kids[c if NEAR_FEED == "direct" else h1] += near
+        key = {c: (0, 0)}
+        todo = [c]
+        while todo:
+            s = todo.pop()
+            for d in kids.get(s, []):
+                key[d] = (key[s][0] + 1, key[s][1] + (topo.chip(s) != topo.chip(d)))
+                todo.append(d)
+        tree.append(kids)
+        due.append(key)
+    return tree, due
+
+
+def _calls(T, topo, tree, due, s):
+    own = T.rank_of(s)
+    groups = []
+    passed = sorted([j for j in range(N) if j != own and tree[j].get(s)], key=lambda j: (due[j][s], j))
+    if own is not None:
+        groups.append([own])
+    for j in passed:
+        if FUSE_PASS and len(groups) > (own is not None) and due[groups[-1][0]][s][0] == due[j][s][0]:
+            groups[-1].append(j)
+        else:
+            groups.append([j])
+    out = []
+    for grp in groups:
+        ent = [(j, d) for j in grp for d in tree[j][s]]
+        eng = _split(topo, s, [d for j, d in ent])
+        out.append([(j, d, e) for (j, d), e in zip(ent, eng)])
+    return out
+
+
+def rank_program(g, core, T, topo):
+    tree, due = _plan(T, topo)
+    cores = list(T.cores)
+    rank = T.rank_of(core)
+    if rank is None and not any(core in t for t in tree):
+        return
+    u8 = dt.uint8
+    total, seen = {}, {}
+
+    def inc(ins, name, v):
+        ins.then_inc(T.sem[name], v)
+        total[name] = total.get(name, 0) + v
+
+    def wait(q, qn, name, v):
+        if seen.get((qn, name), 0) < v:
+            q.wait_ge(T.sem[name], v)
+            seen[(qn, name)] = v
+
+    def cw(k):
+        return slice(OFF[k], OFF[k + 1])
+
+    def ce(k):
+        return slice(4 * OFF[k], 4 * OFF[k + 1])
+
+    def dst_id(d):
+        a = topo.addr(d)
+        return DstId(rid=a[0], pnc=a[1])
+
+    if WHOLE:
+        pieces = [("c", 0), ("s", 0)] + [("c", k) for k in range(1, K)]
+    else:
+        pieces = [(p, k) for k in range(K) for p in ("c", "s")]
+
+    def plane_of(k):
+        return 0 if WHOLE else k
+
+    lands = {}
+    for s in sorted({s for t in tree for s in t}):
+        for call in _calls(T, topo, tree, due, s):
+            for j, d, e in call:
+                if d == core:
+                    lands[j] = len(e)
+                    for p, k in pieces:
+                        total["%s%d_%d" % (p, j, k)] = len(e)
+
+    def send_x(call, p, k):
+        trs = []
+        for j, d, e in call:
+            if p == "c":
+                ap = T["xq%d" % j][:, cw(k)].bitcast(u8)
+            elif WHOLE:
+                ap = T["xs%d" % j][:, 0:NC]
+            else:
+                ap = T["xs%d" % j][:, cw(k)]
+            trs.append(RemoteDMATransfer(dst_ids=[dst_id(d)], dma_engine_mask=_tomask(e),
+                                         remote_sem=T.sem["%s%d_%d" % (p, j, k)], src=ap, dst=ap))
+            total["ls"] = total.get("ls", 0) + len(e)
+        g.remote_dma_fused(trs, local_sem=T.sem["ls"])
+
+    def finish():
+        for name in sorted(total):
+            if max([v for (q, s), v in seen.items() if s == name] + [0]) < total[name]:
+                wait(g, "g", name, total[name])
+
+    mine = _calls(T, topo, tree, due, core)
+
+    def pass_on(calls):
+        for call in calls:
+            for p, k in pieces:
+                for j in sorted({j for j, d, e in call}):
+                    wait(g, "g", "%s%d_%d" % (p, j, k), lands[j])
+                send_x(call, p, k)
+
+    if rank is None:
+        pass_on(mine)
+        finish()
+        return
+
+    V, PE, ACT, SY = g.vector, g.tensor, g.scalar, g.sync
+    Copy = ActivationFunctionType.Copy
+    order = sorted(range(N), key=lambda j: (due[j][core], j))
+    XQ = [T["xq%d" % j] for j in range(N)]
+    XS = [T["xs%d" % j] for j in range(N)]
+    ACC, MX, MN = [T.acc0, T.acc1], [T.mx0, T.mx1], [T.mn0, T.mn1]
+    prev = cores[(rank - 1) % N]
+    nxt = cores[(rank + 1) % N]
+    h_mask = _split(topo, core, [prev])[0]
+    h_eng = len(h_mask)
+    h_due = 2 * len(_split(topo, nxt, [core])[0])
+    for k in range(K):
+        total["b%d" % k] = h_due
+
+    steps = [(a, k) for a in range(N) for k in range(K)]
+    at = {s: t for t, s in enumerate(steps)}
+
+    def bank(a, k, i):
+        t = at[(a, k)]
+        return 2 * (t % NPAIR) + i, t // NPAIR
+
+    def pv(b, k):
+        return T.ps[:, 512 * b:512 * b + CH[k]]
+
+    for k in range(K):
+        inc(SY.dma_start(T.xb[:, ce(k)], T.x[:, ce(k)]), "lx%d" % k, 16)
+    wait(ACT, "act", "lx0", 16)
+    inc(ACT.dma_start(T.w1b[:], T.w1[:]), "lw1", 16)
+    inc(ACT.dma_start(T.w2b[:], T.w2[:]), "lw2", 16)
+
+    for p, k in pieces:
+        for kk in (range(K) if (p == "s" and WHOLE) else [k]):
+            wait(g, "g", "qx%d" % kk, 1)
+        send_x(mine[0], p, k)
+    pass_on(mine[1:])
+    for k in range(K):
+        wait(g, "g", "qh%d" % k, 1)
+        a = topo.addr(prev)
+        for src, dst in ((T.hq[:, cw(k)].bitcast(u8), T.hqi[:, cw(k)].bitcast(u8)),
+                         (T.hs[:, cw(k)], T.hsi[:, cw(k)])):
+            g.remote_dma(dst, src, T.sem["b%d" % k], T.sem["hl%d" % k], a[1], a[0], _tomask(h_mask))
+            total["hl%d" % k] = total.get("hl%d" % k, 0) + h_eng
+
+    wait(PE, "pe", "qw1", 1)
+
+    def y_own(k):
+        wait(PE, "pe", "qw2", 1)
+        wait(PE, "pe", "qh%d" % k, 1)
+        PE.matmul_mx(pv(2 * NPAIR + k, k), T.w2q[:, 0:128], T.w2s[:, 0:128], T.hq[:, cw(k)], T.hs[:, cw(k)],
+                     True, False)
+
+    for a, k in steps:
+        j = order[a]
+        if a == 0:
+            wait(PE, "pe", "qx%d" % k, 1)
+        else:
+            wait(PE, "pe", "s%d_%d" % (j, plane_of(k)), lands[j])
+            wait(PE, "pe", "c%d_%d" % (j, k), lands[j])
+        for i in range(2):
+            b, u = bank(a, k, i)
+            wait(PE, "pe", "rel%d" % b, 2 * u)
+            inc(PE.matmul_mx(pv(b, k), T.w1q[:, 128 * i:128 * i + 128], T.w1s[:, 128 * i:128 * i + 128],
+                             XQ[j][:, cw(k)], XS[j][:, cw(k)], True, True), "mm%d" % b, 1)
+        if a == N - 1 and k:
+            y_own(k - 1)
+    y_own(K - 1)
+    for k in range(K):
+        wait(PE, "pe", "b%d" % k, h_due)
+        inc(PE.matmul_mx(pv(2 * NPAIR + k, k), T.w2q[:, 128:256], T.w2s[:, 128:256], T.hqi[:, cw(k)],
+                         T.hsi[:, cw(k)], False, True), "ym%d" % k, 1)
+
+    def hcol(k, c):
+        return T.hb[:, 4 * OFF[k] + c:4 * OFF[k + 1]:4]
+
+    for k in range(K):
+        wait(V, "v", "lx%d" % k, 16)
+        inc(V.quantize_mx(XQ[rank][:, cw(k)], XS[rank][:, cw(k)], T.xb[:, ce(k)]), "qx%d" % k, 1)
+    wait(V, "v", "lw1", 16)
+    inc(V.quantize_mx(T.w1q[:], T.w1s[:], T.w1b[:]), "qw1", 1)
+    for a in range(1, N):
+        if a == N - 1:
+            wait(V, "v", "lw2", 16)
+            inc(V.quantize_mx(T.w2q[:], T.w2s[:], T.w2b[:]), "qw2", 1)
+        for k in range(K):
+            for i in range(2):
+                b, u = bank(a, k, i)
+                pb, pu = bank(a - 1, k, i)
+                wait(V, "v", "mm%d" % b, u + 1)
+                wait(V, "v", "rel%d" % pb, 2 * pu + 2)
+                hi, lo = (ACC[i], ACC[i]) if a == 1 else (MX[i], MN[i])
+                inc(V.tensor_tensor(MX[i][:, cw(k)], hi[:, cw(k)], pv(b, k), AluOpType.max), "rel%d" % b, 1)
+                inc(V.tensor_tensor(MN[i][:, cw(k)], lo[:, cw(k)], pv(b, k), AluOpType.min), "rel%d" % b, 1)
+            if a == N - 1:
+                if V_SCALES:
+                    wait(V, "v", "rel%d" % b, 2 * u + 2)
+                    inc(V.tensor_scalar(hcol(k, 3), MN[1][:, cw(k)], CONST, None, AluOpType.mult), "hsc%d" % k, 1)
+                wait(V, "v", "hsc%d" % k, 4)
+                inc(V.quantize_mx(T.hq[:, cw(k)], T.hs[:, cw(k)], T.hb[:, ce(k)]), "qh%d" % k, 1)
+
+    for k in range(K):
+        for i in range(2):
+            b, u = bank(0, k, i)
+            wait(ACT, "act", "mm%d" % b, u + 1)
+            inc(ACT.activation(ACC[i][:, cw(k)], pv(b, k), Copy), "rel%d" % b, 2)
+    for k in range(K):
+        for c, buf in ((0, MX[0]), (1, MN[0]), (2, MX[1]), (3, MN[1]))[:3 if V_SCALES else 4]:
+            b, u = bank(N - 1, k, c // 2)
+            wait(ACT, "act", "rel%d" % b, 2 * u + 2)
+            inc(ACT.activation(hcol(k, c), buf[:, cw(k)], Copy, scale=CONST), "hsc%d" % k, 1)
+    for k in range(K):
+        wait(ACT, "act", "ym%d" % k, 1)
+        inc(ACT.activation(T.yb[:, cw(k)], pv(2 * NPAIR + k, k), Copy), "ye%d" % k, 1)
+        wait(ACT, "act", "ye%d" % k, 1)
+        inc(ACT.dma_start(T.y[:, cw(k)], T.yb[:, cw(k)]), "sty", 16)
+
+    for k in range(K):
+        wait(SY, "sy", "hsc%d" % k, 4)
+        for kk in ([K - 1, k] if H_STORE_LAST else [k]):
+            wait(SY, "sy", "hl%d" % kk, 2 * h_eng)
+        inc(SY.dma_start(T.h[:, ce(k)], T.hb[:, ce(k)]), "sth", 16)
+    finish()

@@ -4,18 +4,9 @@ from concourse.mybir import dt, AluOpType, ActivationFunctionType
 
 N = 4
 NC = 512
-CH = [256, 256]
+CH = [128, 256, 128]
 K = len(CH)
 OFF = [sum(CH[:k]) for k in range(K + 1)]
-WHOLE = True
-OWNER_FAR = "fwd"
-OTHER_FAR = "gate"
-NEAR_FEED = "direct"
-FUSE_PASS = True
-H_STORE_LAST = True
-V_SCALES = True
-FAR_ENG = 16
-NEAR_ENG = 16
 NPAIR = (8 - K) // 2
 CONST = float(np.float32(0.047))
 
@@ -73,16 +64,15 @@ def _split(topo, src, dsts):
     taken = []
     if far:
         pool = _bits(topo.mask(src, dsts[far[0]]))
-        c = min(_pow2(len(pool) // len(far)), FAR_ENG)
+        c = _pow2(len(pool) // len(far))
         for n, i in enumerate(far):
             out[i] = pool[c * n:c * n + c]
         taken = pool
     if near:
         pool = [e for e in _bits(topo.mask(src, dsts[near[0]])) if e not in taken]
-        c = min(_pow2(len(pool) // len(near)), NEAR_ENG)
-        sizes = [c] * len(near)
+        sizes = [_pow2(len(pool) // len(near))] * len(near)
         for n in range(len(near)):
-            if sum(sizes) + sizes[n] <= len(pool) and 2 * sizes[n] <= NEAR_ENG:
+            if sum(sizes) + sizes[n] <= len(pool):
                 sizes[n] *= 2
         at = 0
         for i, s in zip(near, sizes):
@@ -100,45 +90,26 @@ def _plan(T, topo):
     def hurried(d):
         return topo.chip(cores[(cores.index(d) - 1) % N]) != topo.chip(d)
 
-    def helper(c, d, at_mate):
-        if at_mate:
-            q = [q for q in everyone if q not in busy and topo.mates(topo.chip(q), topo.chip(d))
-                 and topo.same_plane(topo.chip(q), topo.chip(c)) and topo.die(q) == topo.die(c)
-                 and topo.may_write(q, d)][0]
-        else:
-            q = [q for q in everyone if q not in busy and topo.chip(q) == topo.chip(c)
-                 and topo.die(q) == topo.die(c) and topo.may_write(q, d)][0]
+    def helper(c, d):
+        q = [q for q in everyone if q not in busy and topo.chip(q) == topo.chip(c)
+             and topo.die(q) == topo.die(c) and topo.may_write(q, d)][0]
         busy.append(q)
         return q
 
     for c in cores:
-        kids = {c: []}
         near = [d for d in cores if d != c and topo.chip(d) == topo.chip(c)]
         far = sorted([d for d in cores if topo.chip(d) != topo.chip(c)], key=lambda d: not hurried(d))
+        kids = {c: []}
         if all(topo.may_write(c, d) for d in far):
             kids[c] += near
-            if OWNER_FAR == "fwd":
-                kids[c].append(far[0])
-                kids[far[0]] = far[1:]
-            else:
-                kids[c] += far
-        elif OTHER_FAR == "chain":
-            kids = {c: near, [d for d in near if topo.may_write(d, far[0])][0]: [far[0]], far[0]: [far[1]]}
+            kids[c].append(far[0])
+            kids[far[0]] = far[1:]
         else:
-            h1 = helper(c, far[0], False)
-            kids[c].append(h1)
-            kids[h1] = [far[0]]
-            if OTHER_FAR in ("mate", "same"):
-                h2 = helper(c, far[1], OTHER_FAR == "mate")
-                kids[c].append(h2)
-                kids[h2] = [far[1]]
-            elif OTHER_FAR == "h1dup":
-                kids[h1].append(far[1])
-            elif OTHER_FAR == "gate":
-                kids[[d for d in near if topo.may_write(d, far[1])][0]] = [far[1]]
-            else:
-                kids[far[0]] = [far[1]]
-            kids[c if NEAR_FEED == "direct" else h1] += near
+            q = helper(c, far[0])
+            kids[c].append(q)
+            kids[c] += near
+            kids[q] = [far[0]]
+            kids[[d for d in near if topo.may_write(d, far[1])][0]] = [far[1]]
         key = {c: (0, 0)}
         todo = [c]
         while todo:
@@ -158,7 +129,7 @@ def _calls(T, topo, tree, due, s):
     if own is not None:
         groups.append([own])
     for j in passed:
-        if FUSE_PASS and len(groups) > (own is not None) and due[groups[-1][0]][s][0] == due[j][s][0]:
+        if len(groups) > (own is not None) and due[groups[-1][0]][s][0] == due[j][s][0]:
             groups[-1].append(j)
         else:
             groups.append([j])
@@ -198,13 +169,7 @@ def rank_program(g, core, T, topo):
         a = topo.addr(d)
         return DstId(rid=a[0], pnc=a[1])
 
-    if WHOLE:
-        pieces = [("c", 0), ("s", 0)] + [("c", k) for k in range(1, K)]
-    else:
-        pieces = [(p, k) for k in range(K) for p in ("c", "s")]
-
-    def plane_of(k):
-        return 0 if WHOLE else k
+    pieces = [("c", 0), ("s", 0)] + [("c", k) for k in range(1, K)]
 
     lands = {}
     for s in sorted({s for t in tree for s in t}):
@@ -218,12 +183,7 @@ def rank_program(g, core, T, topo):
     def send_x(call, p, k):
         trs = []
         for j, d, e in call:
-            if p == "c":
-                ap = T["xq%d" % j][:, cw(k)].bitcast(u8)
-            elif WHOLE:
-                ap = T["xs%d" % j][:, 0:NC]
-            else:
-                ap = T["xs%d" % j][:, cw(k)]
+            ap = T["xq%d" % j][:, cw(k)].bitcast(u8) if p == "c" else T["xs%d" % j][:, 0:NC]
             trs.append(RemoteDMATransfer(dst_ids=[dst_id(d)], dma_engine_mask=_tomask(e),
                                          remote_sem=T.sem["%s%d_%d" % (p, j, k)], src=ap, dst=ap))
             total["ls"] = total.get("ls", 0) + len(e)
@@ -278,10 +238,15 @@ def rank_program(g, core, T, topo):
     inc(ACT.dma_start(T.w1b[:], T.w1[:]), "lw1", 16)
     inc(ACT.dma_start(T.w2b[:], T.w2[:]), "lw2", 16)
 
-    for p, k in pieces:
-        for kk in (range(K) if (p == "s" and WHOLE) else [k]):
+    ahead = [t for t in mine[0] if T.rank_of(t[1]) is None]
+    for n, (p, k) in enumerate(pieces):
+        for kk in (range(K) if p == "s" else [k]):
             wait(g, "g", "qx%d" % kk, 1)
-        send_x(mine[0], p, k)
+        if n == 0 and ahead:
+            send_x(ahead, p, k)
+            send_x([t for t in mine[0] if t not in ahead], p, k)
+        else:
+            send_x(mine[0], p, k)
     pass_on(mine[1:])
     for k in range(K):
         wait(g, "g", "qh%d" % k, 1)
@@ -304,7 +269,7 @@ def rank_program(g, core, T, topo):
         if a == 0:
             wait(PE, "pe", "qx%d" % k, 1)
         else:
-            wait(PE, "pe", "s%d_%d" % (j, plane_of(k)), lands[j])
+            wait(PE, "pe", "s%d_0" % j, lands[j])
             wait(PE, "pe", "c%d_%d" % (j, k), lands[j])
         for i in range(2):
             b, u = bank(a, k, i)
@@ -327,25 +292,24 @@ def rank_program(g, core, T, topo):
         inc(V.quantize_mx(XQ[rank][:, cw(k)], XS[rank][:, cw(k)], T.xb[:, ce(k)]), "qx%d" % k, 1)
     wait(V, "v", "lw1", 16)
     inc(V.quantize_mx(T.w1q[:], T.w1s[:], T.w1b[:]), "qw1", 1)
-    for a in range(1, N):
+    wait(V, "v", "lw2", 16)
+    inc(V.quantize_mx(T.w2q[:], T.w2s[:], T.w2b[:]), "qw2", 1)
+    for a, k in steps:
+        if a == 0:
+            continue
+        for i in range(2):
+            b, u = bank(a, k, i)
+            pb, pu = bank(a - 1, k, i)
+            wait(V, "v", "mm%d" % b, u + 1)
+            wait(V, "v", "rel%d" % pb, 2 * pu + 2)
+            hi, lo = (ACC[i], ACC[i]) if a == 1 else (MX[i], MN[i])
+            inc(V.tensor_tensor(MX[i][:, cw(k)], hi[:, cw(k)], pv(b, k), AluOpType.max), "rel%d" % b, 1)
+            inc(V.tensor_tensor(MN[i][:, cw(k)], lo[:, cw(k)], pv(b, k), AluOpType.min), "rel%d" % b, 1)
         if a == N - 1:
-            wait(V, "v", "lw2", 16)
-            inc(V.quantize_mx(T.w2q[:], T.w2s[:], T.w2b[:]), "qw2", 1)
-        for k in range(K):
-            for i in range(2):
-                b, u = bank(a, k, i)
-                pb, pu = bank(a - 1, k, i)
-                wait(V, "v", "mm%d" % b, u + 1)
-                wait(V, "v", "rel%d" % pb, 2 * pu + 2)
-                hi, lo = (ACC[i], ACC[i]) if a == 1 else (MX[i], MN[i])
-                inc(V.tensor_tensor(MX[i][:, cw(k)], hi[:, cw(k)], pv(b, k), AluOpType.max), "rel%d" % b, 1)
-                inc(V.tensor_tensor(MN[i][:, cw(k)], lo[:, cw(k)], pv(b, k), AluOpType.min), "rel%d" % b, 1)
-            if a == N - 1:
-                if V_SCALES:
-                    wait(V, "v", "rel%d" % b, 2 * u + 2)
-                    inc(V.tensor_scalar(hcol(k, 3), MN[1][:, cw(k)], CONST, None, AluOpType.mult), "hsc%d" % k, 1)
-                wait(V, "v", "hsc%d" % k, 4)
-                inc(V.quantize_mx(T.hq[:, cw(k)], T.hs[:, cw(k)], T.hb[:, ce(k)]), "qh%d" % k, 1)
+            wait(V, "v", "rel%d" % b, 2 * u + 2)
+            inc(V.tensor_scalar(hcol(k, 3), MN[1][:, cw(k)], CONST, None, AluOpType.mult), "hsc%d" % k, 1)
+            wait(V, "v", "hsc%d" % k, 4)
+            inc(V.quantize_mx(T.hq[:, cw(k)], T.hs[:, cw(k)], T.hb[:, ce(k)]), "qh%d" % k, 1)
 
     for k in range(K):
         for i in range(2):
@@ -353,7 +317,7 @@ def rank_program(g, core, T, topo):
             wait(ACT, "act", "mm%d" % b, u + 1)
             inc(ACT.activation(ACC[i][:, cw(k)], pv(b, k), Copy), "rel%d" % b, 2)
     for k in range(K):
-        for c, buf in ((0, MX[0]), (1, MN[0]), (2, MX[1]), (3, MN[1]))[:3 if V_SCALES else 4]:
+        for c, buf in ((0, MX[0]), (1, MN[0]), (2, MX[1])):
             b, u = bank(N - 1, k, c // 2)
             wait(ACT, "act", "rel%d" % b, 2 * u + 2)
             inc(ACT.activation(hcol(k, c), buf[:, cw(k)], Copy, scale=CONST), "hsc%d" % k, 1)
@@ -365,7 +329,6 @@ def rank_program(g, core, T, topo):
 
     for k in range(K):
         wait(SY, "sy", "hsc%d" % k, 4)
-        for kk in ([K - 1, k] if H_STORE_LAST else [k]):
-            wait(SY, "sy", "hl%d" % kk, 2 * h_eng)
-        inc(SY.dma_start(T.h[:, ce(k)], T.hb[:, ce(k)]), "sth", 16)
+        wait(SY, "sy", "hl%d" % k, 2 * h_eng)
+    inc(SY.dma_start(T.h[:], T.hb[:]), "sth", 16)
     finish()

import numpy as np
from concourse.bass import DstId, RemoteDMATransfer
from concourse.mybir import dt, AluOpType, ActivationFunctionType

N = 4
NC = 512
CH = [128, 256, 128]
K = len(CH)
OFF = [sum(CH[:k]) for k in range(K + 1)]
NPAIR = (8 - K) // 2
CONST = float(np.float32(0.047))

SCRATCH = {
    "xb": ("sbuf", [128, 4 * NC], "bfloat16"),
    "w1b": ("sbuf", [128, 1024], "bfloat16"),
    "w2b": ("sbuf", [128, 1024], "bfloat16"),
    "w1q": ("sbuf", [128, 256], "float8_e4m3fn_x4"),
    "w1s": ("sbuf", [128, 256], "uint8"),
    "w2q": ("sbuf", [128, 256], "float8_e4m3fn_x4"),
    "w2s": ("sbuf", [128, 256], "uint8"),
    "hb": ("sbuf", [128, 4 * NC], "bfloat16"),
    "hq": ("sbuf", [128, NC], "float8_e4m3fn_x4"),
    "hs": ("sbuf", [128, NC], "uint8"),
    "hqi": ("sbuf", [128, NC], "float8_e4m3fn_x4"),
    "hsi": ("sbuf", [128, NC], "uint8"),
    "yb": ("sbuf", [128, NC], "float32"),
    "ps": ("psum", [128, 8 * 512], "float32"),
}
for _j in range(N):
    SCRATCH["xq%d" % _j] = ("sbuf", [128, NC], "float8_e4m3fn_x4")
    SCRATCH["xs%d" % _j] = ("sbuf", [128, NC], "uint8")
for _i in range(2):
    for _nm in ("acc", "mx", "mn"):
        SCRATCH["%s%d" % (_nm, _i)] = ("sbuf", [128, NC], "float32")

SEMAPHORES = (["lw1", "lw2", "qw1", "qw2", "ls", "sth", "sty"]
              + ["%s%d" % (p, k) for p in ("lx", "qx", "b", "hsc", "qh", "hl", "ym", "ye") for k in range(K)]
              + ["%s%d_%d" % (p, j, k) for p in ("c", "s") for j in range(N) for k in range(K)]
              + ["%s%d" % (p, b) for p in ("mm", "rel") for b in range(2 * NPAIR)])


def _bits(m):
    return [e for e in range(16) if (m >> e) & 1]


def _pow2(v):
    p = 1
    while 2 * p <= v:
        p *= 2
    return p


def _tomask(engines):
    m = 0
    for e in engines:
        m |= 1 << e
    return m


def _split(topo, src, dsts):
    far = [i for i, d in enumerate(dsts) if topo.chip(d) != topo.chip(src)]
    near = [i for i, d in enumerate(dsts) if topo.chip(d) == topo.chip(src)]
    out = [None] * len(dsts)
    taken = []
    if far:
        pool = _bits(topo.mask(src, dsts[far[0]]))
        c = _pow2(len(pool) // len(far))
        for n, i in enumerate(far):
            out[i] = pool[c * n:c * n + c]
        taken = pool
    if near:
        pool = [e for e in _bits(topo.mask(src, dsts[near[0]])) if e not in taken]
        sizes = [_pow2(len(pool) // len(near))] * len(near)
        for n in range(len(near)):
            if sum(sizes) + sizes[n] <= len(pool):
                sizes[n] *= 2
        at = 0
        for i, s in zip(near, sizes):
            out[i] = pool[at:at + s]
            at += s
    return out


def _plan(T, topo):
    cores = list(T.cores)
    everyone = range(topo.CORES_PER_CHIP * topo.CHIPS)
    busy = list(cores)
    tree, due = [], []

    def hurried(d):
        return topo.chip(cores[(cores.index(d) - 1) % N]) != topo.chip(d)

    def helper(c, d):
        q = [q for q in everyone if q not in busy and topo.chip(q) == topo.chip(c)
             and topo.die(q) == topo.die(c) and topo.may_write(q, d)][0]
        busy.append(q)
        return q

    for c in cores:
        near = [d for d in cores if d != c and topo.chip(d) == topo.chip(c)]
        far = sorted([d for d in cores if topo.chip(d) != topo.chip(c)], key=lambda d: not hurried(d))
        kids = {c: []}
        if all(topo.may_write(c, d) for d in far):
            kids[c] += near
            kids[c].append(far[0])
            kids[far[0]] = far[1:]
        else:
            q = helper(c, far[0])
            kids[c].append(q)
            kids[c] += near
            kids[q] = [far[0]]
            kids[[d for d in near if topo.may_write(d, far[1])][0]] = [far[1]]
        key = {c: (0, 0)}
        todo = [c]
        while todo:
            s = todo.pop()
            for d in kids.get(s, []):
                key[d] = (key[s][0] + 1, key[s][1] + (topo.chip(s) != topo.chip(d)))
                todo.append(d)
        tree.append(kids)
        due.append(key)
    return tree, due


def _calls(T, topo, tree, due, s):
    own = T.rank_of(s)
    groups = []
    passed = sorted([j for j in range(N) if j != own and tree[j].get(s)], key=lambda j: (due[j][s], j))
    if own is not None:
        groups.append([own])
    for j in passed:
        if len(groups) > (own is not None) and due[groups[-1][0]][s][0] == due[j][s][0]:
            groups[-1].append(j)
        else:
            groups.append([j])
    out = []
    for grp in groups:
        ent = [(j, d) for j in grp for d in tree[j][s]]
        eng = _split(topo, s, [d for j, d in ent])
        out.append([(j, d, e) for (j, d), e in zip(ent, eng)])
    return out


def rank_program(g, core, T, topo):
    tree, due = _plan(T, topo)
    cores = list(T.cores)
    rank = T.rank_of(core)
    if rank is None and not any(core in t for t in tree):
        return
    u8 = dt.uint8
    total, seen = {}, {}

    def inc(ins, name, v):
        ins.then_inc(T.sem[name], v)
        total[name] = total.get(name, 0) + v

    def wait(q, qn, name, v):
        if seen.get((qn, name), 0) < v:
            q.wait_ge(T.sem[name], v)
            seen[(qn, name)] = v

    def cw(k):
        return slice(OFF[k], OFF[k + 1])

    def ce(k):
        return slice(4 * OFF[k], 4 * OFF[k + 1])

    def dst_id(d):
        a = topo.addr(d)
        return DstId(rid=a[0], pnc=a[1])

    pieces = [("c", 0), ("s", 0)] + [("c", k) for k in range(1, K)]

    lands = {}
    for s in sorted({s for t in tree for s in t}):
        for call in _calls(T, topo, tree, due, s):
            for j, d, e in call:
                if d == core:
                    lands[j] = len(e)
                    for p, k in pieces:
                        total["%s%d_%d" % (p, j, k)] = len(e)

    def send_x(call, p, k):
        trs = []
        for j, d, e in call:
            ap = T["xq%d" % j][:, cw(k)].bitcast(u8) if p == "c" else T["xs%d" % j][:, 0:NC]
            trs.append(RemoteDMATransfer(dst_ids=[dst_id(d)], dma_engine_mask=_tomask(e),
                                         remote_sem=T.sem["%s%d_%d" % (p, j, k)], src=ap, dst=ap))
            total["ls"] = total.get("ls", 0) + len(e)
        g.remote_dma_fused(trs, local_sem=T.sem["ls"])

    def finish():
        for name in sorted(total):
            if max([v for (q, s), v in seen.items() if s == name] + [0]) < total[name]:
                wait(g, "g", name, total[name])

    mine = _calls(T, topo, tree, due, core)

    def pass_on(calls):
        for call in calls:
            for p, k in pieces:
                for j in sorted({j for j, d, e in call}):
                    wait(g, "g", "%s%d_%d" % (p, j, k), lands[j])
                send_x(call, p, k)

    if rank is None:
        pass_on(mine)
        finish()
        return

    V, PE, ACT, SY = g.vector, g.tensor, g.scalar, g.sync
    Copy = ActivationFunctionType.Copy
    order = sorted(range(N), key=lambda j: (due[j][core], j))
    XQ = [T["xq%d" % j] for j in range(N)]
    XS = [T["xs%d" % j] for j in range(N)]
    ACC, MX, MN = [T.acc0, T.acc1], [T.mx0, T.mx1], [T.mn0, T.mn1]
    prev = cores[(rank - 1) % N]
    nxt = cores[(rank + 1) % N]
    h_mask = _split(topo, core, [prev])[0]
    h_eng = len(h_mask)
    h_due = 2 * len(_split(topo, nxt, [core])[0])
    for k in range(K):
        total["b%d" % k] = h_due

    steps = [(a, k) for a in range(N) for k in range(K)]
    at = {s: t for t, s in enumerate(steps)}

    def bank(a, k, i):
        t = at[(a, k)]
        return 2 * (t % NPAIR) + i, t // NPAIR

    def pv(b, k):
        return T.ps[:, 512 * b:512 * b + CH[k]]

    for k in range(K):
        inc(SY.dma_start(T.xb[:, ce(k)], T.x[:, ce(k)]), "lx%d" % k, 16)
    wait(ACT, "act", "lx0", 16)
    inc(ACT.dma_start(T.w1b[:], T.w1[:]), "lw1", 16)
    inc(ACT.dma_start(T.w2b[:], T.w2[:]), "lw2", 16)

    ahead = [t for t in mine[0] if T.rank_of(t[1]) is None]
    for n, (p, k) in enumerate(pieces):
        for kk in (range(K) if p == "s" else [k]):
            wait(g, "g", "qx%d" % kk, 1)
        if n == 0 and ahead:
            send_x(ahead, p, k)
            send_x([t for t in mine[0] if t not in ahead], p, k)
        else:
            send_x(mine[0], p, k)
    pass_on(mine[1:])
    for k in range(K):
        wait(g, "g", "qh%d" % k, 1)
        a = topo.addr(prev)
        for src, dst in ((T.hq[:, cw(k)].bitcast(u8), T.hqi[:, cw(k)].bitcast(u8)),
                         (T.hs[:, cw(k)], T.hsi[:, cw(k)])):
            g.remote_dma(dst, src, T.sem["b%d" % k], T.sem["hl%d" % k], a[1], a[0], _tomask(h_mask))
            total["hl%d" % k] = total.get("hl%d" % k, 0) + h_eng

    wait(PE, "pe", "qw1", 1)

    def y_own(k):
        wait(PE, "pe", "qw2", 1)
        wait(PE, "pe", "qh%d" % k, 1)
        PE.matmul_mx(pv(2 * NPAIR + k, k), T.w2q[:, 0:128], T.w2s[:, 0:128], T.hq[:, cw(k)], T.hs[:, cw(k)],
                     True, False)

    for a, k in steps:
        j = order[a]
        if a == 0:
            wait(PE, "pe", "qx%d" % k, 1)
        else:
            wait(PE, "pe", "s%d_0" % j, lands[j])
            wait(PE, "pe", "c%d_%d" % (j, k), lands[j])
        for i in range(2):
            b, u = bank(a, k, i)
            wait(PE, "pe", "rel%d" % b, 2 * u)
            inc(PE.matmul_mx(pv(b, k), T.w1q[:, 128 * i:128 * i + 128], T.w1s[:, 128 * i:128 * i + 128],
                             XQ[j][:, cw(k)], XS[j][:, cw(k)], True, True), "mm%d" % b, 1)
        if a == N - 1 and k:
            y_own(k - 1)
    y_own(K - 1)
    for k in range(K):
        wait(PE, "pe", "b%d" % k, h_due)
        inc(PE.matmul_mx(pv(2 * NPAIR + k, k), T.w2q[:, 128:256], T.w2s[:, 128:256], T.hqi[:, cw(k)],
                         T.hsi[:, cw(k)], False, True), "ym%d" % k, 1)

    def hcol(k, c):
        return T.hb[:, 4 * OFF[k] + c:4 * OFF[k + 1]:4]

    for k in range(K):
        wait(V, "v", "lx%d" % k, 16)
        inc(V.quantize_mx(XQ[rank][:, cw(k)], XS[rank][:, cw(k)], T.xb[:, ce(k)]), "qx%d" % k, 1)
    wait(V, "v", "lw1", 16)
    inc(V.quantize_mx(T.w1q[:], T.w1s[:], T.w1b[:]), "qw1", 1)
    wait(V, "v", "lw2", 16)
    inc(V.quantize_mx(T.w2q[:], T.w2s[:], T.w2b[:]), "qw2", 1)
    for a, k in steps:
        if a == 0:
            continue
        for i in range(2):
            b, u = bank(a, k, i)
            pb, pu = bank(a - 1, k, i)
            wait(V, "v", "mm%d" % b, u + 1)
            wait(V, "v", "rel%d" % pb, 2 * pu + 2)
            hi, lo = (ACC[i], ACC[i]) if a == 1 else (MX[i], MN[i])
            inc(V.tensor_tensor(MX[i][:, cw(k)], hi[:, cw(k)], pv(b, k), AluOpType.max), "rel%d" % b, 1)
            inc(V.tensor_tensor(MN[i][:, cw(k)], lo[:, cw(k)], pv(b, k), AluOpType.min), "rel%d" % b, 1)
        if a == N - 1:
            wait(V, "v", "rel%d" % b, 2 * u + 2)
            inc(V.tensor_scalar(hcol(k, 3), MN[1][:, cw(k)], CONST, None, AluOpType.mult), "hsc%d" % k, 1)
            wait(V, "v", "hsc%d" % k, 4)
            inc(V.quantize_mx(T.hq[:, cw(k)], T.hs[:, cw(k)], T.hb[:, ce(k)]), "qh%d" % k, 1)

    for k in range(K):
        for i in range(2):
            b, u = bank(0, k, i)
            wait(ACT, "act", "mm%d" % b, u + 1)
            inc(ACT.activation(ACC[i][:, cw(k)], pv(b, k), Copy), "rel%d" % b, 2)
    for k in range(K):
        for c, buf in ((0, MX[0]), (1, MN[0]), (2, MX[1])):
            b, u = bank(N - 1, k, c // 2)
            wait(ACT, "act", "rel%d" % b, 2 * u + 2)
            inc(ACT.activation(hcol(k, c), buf[:, cw(k)], Copy, scale=CONST), "hsc%d" % k, 1)
    for k in range(K):
        wait(ACT, "act", "ym%d" % k, 1)
        inc(ACT.activation(T.yb[:, cw(k)], pv(2 * NPAIR + k, k), Copy), "ye%d" % k, 1)
        wait(ACT, "act", "ye%d" % k, 1)
        inc(ACT.dma_start(T.y[:, cw(k)], T.yb[:, cw(k)]), "sty", 16)

    for k in range(K):
        wait(SY, "sy", "hsc%d" % k, 4)
        wait(SY, "sy", "hl%d" % k, 2 * h_eng)
    inc(SY.dma_start(T.h[:], T.hb[:]), "sth", 16)
    finish()
